import numpy as np
import ml_dtypes


def mxq(x, axis, fmt="e4m3"):
    dtype, down = {"e4m3": (ml_dtypes.float8_e4m3fn, 7), "e5m2": (ml_dtypes.float8_e5m2, 14)}[fmt]
    v = np.moveaxis(np.asarray(x, np.float32).astype(ml_dtypes.bfloat16).astype(np.float64), axis, -1)
    blocks = v.reshape(v.shape[:-1] + (-1, 32))
    amax = np.abs(blocks).max(-1, keepdims=True)
    byte = np.maximum(np.where(amax > 0, np.frexp(amax)[1] - 1 + 127, 0) - down, 1)
    scale = np.exp2(byte - 127.0)
    codes = (blocks / scale).astype(np.float32).astype(dtype).astype(np.float64)
    return np.moveaxis((codes * scale).reshape(v.shape), -1, axis)


WIDE = False


def mx_kscale(k):
    if not WIDE:
        return np.ones(k)
    levels = np.array([10, -10, 5, -5, 0])
    if k % 512:
        return np.exp2(np.random.permutation(np.resize(levels, k // 32))).repeat(32)
    a = np.empty((k // 512, 16))
    for p in range(k // 512):
        a[p, :8] = np.random.permutation(np.resize(levels, 8))
        for g in range(8):
            far = levels[np.abs(levels - a[p, g]) >= 10]
            a[p, g + 8] = far[np.random.randint(len(far))]
    return np.exp2(a.ravel()).repeat(32)


def f64(x):
    return np.asarray(x).astype(np.float64)


def striped(idx):
    return np.tile(idx.reshape(-1, 16).T, (8, 1)).astype(np.uint16)


def unstriped(offs):
    return offs[:16].T.reshape(-1).astype(np.int64)


def silu(v):
    return v / (1.0 + np.exp(-np.maximum(v, -700.0)))


K, T, E, C, H, N = 512, 512, 6, 256, 512, 384
TOP = 3


def by_expert(wq, xq):
    return np.concatenate([wq[e].T @ xq[:, e * C:(e + 1) * C] for e in range(E)], axis=1)


def setup_inputs():
    n = np.random.standard_normal
    s = mx_kscale(K)[:, None]
    u = mx_kscale(H)
    deal = np.repeat(np.arange(E), C).reshape(TOP, T)[:, np.random.permutation(T)]
    deal = np.take_along_axis(deal, np.argsort(np.random.rand(TOP, T), axis=0), axis=0)
    for _ in range(8):
        s_, t_ = np.random.permutation(T).reshape(2, -1); r = np.random.randint(TOP, size=T // 2); x, y = deal[r, s_].copy(), deal[r, t_].copy()
        ok = ~((deal[:, s_] == y).any(0) | (deal[:, t_] == x).any(0)); deal[r[ok], s_[ok]] = y[ok]; deal[r[ok], t_[ok]] = x[ok]
    order = np.lexsort((np.random.rand(TOP * T), deal.reshape(-1)))
    slot_token = order % T; pos = np.empty(TOP * T, np.int64); pos[order] = np.arange(TOP * T); pos = pos.reshape(TOP, T)
    g = np.random.uniform(0.5, 1.5, (TOP, T)); g = g / g.sum(0)
    return {
        "xT": (n((K, T)) * s).astype(np.float32),
        "w1": (n((E, K, H)) / np.sqrt(K) / s[None]).astype(np.float32),
        "w3": (n((E, K, H)) / np.sqrt(K) / s[None] * u[None, None, :]).astype(np.float32),
        "w2": (n((E, H, N)) / np.sqrt(H) / u[None, :, None]).astype(np.float32),
        "gate": np.stack([np.tile(r, (N, 1)) for r in g]).astype(np.float32),
        "offs": striped(slot_token),
        "pos1": striped(pos[0]),
        "pos2": striped(pos[1]),
        "pos3": striped(pos[2]),
    }


def reference(xT, w1, w3, w2, gate, offs, pos1, pos2, pos3):
    idx = unstriped(offs)
    xq = mxq(f64(xT)[:, idx], 0, "e4m3")
    h = silu(by_expert(mxq(f64(w1), 1, "e4m3"), xq))
    h = h * by_expert(mxq(f64(w3), 1, "e4m3"), xq)
    y = by_expert(mxq(f64(w2), 1, "e4m3"), mxq(h, 0, "e4m3"))
    return sum(f64(gate[r]) * y[:, unstriped(p)] for r, p in enumerate((pos1, pos2, pos3)))

@@ -1,0 +1,192 @@
+from contextlib import ExitStack
+
+import concourse.mybir as mybir
+
+K, T, E, C, H, N = 512, 512, 6, 256, 512, 384
+TOP = 3
+FLOPS = 2 * TOP * T * (2 * K * H + H * N)
+
+F32 = mybir.dt.float32
+BF16 = mybir.dt.bfloat16
+U32 = mybir.dt.uint32
+U16 = mybir.dt.uint16
+U8 = mybir.dt.uint8
+FP8X4 = mybir.dt.float8_e4m3fn_x4
+MULT = mybir.AluOpType.mult
+ADD = mybir.AluOpType.add
+SILU = mybir.ActivationFunctionType.Silu
+
+P = 128
+BLK = 128
+GATHER = 384
+S = E * C
+
+MS1 = [80,128,128,128,128,80]
+MS3 = [80,48,48,48,48,80]
+MSX = 40
+MSN = [0,32,32]
+POS = [5,5,6]
+YV = []
+LOADS = [("a", 0), ("b", 0), ("a", 1), ("b", 1), ("a", 2), ("b", 2), ("a", 3), ("b", 3), ("a", 4), ("b", 4), ("a", 5), ("b", 5), ("c", 0), ("c", 1), ("c", 2), ("c", 3), ("n", 4), ("n", 5), ("g", 0), ("m", 4), ("m", 5), ("g", 1), ("g", 2)]
+GATH = {0: [0], 1: [1], 3: [2], 4: [3]}
+RING = 10
+QPAIR = []
+
+
+def tile_moe_tk_glu_silu_kernel(tc, xT, w1, w3, w2, gate, offs, pos1, pos2, pos3, out):
+    nc = tc.nc
+    with ExitStack() as ctx:
+        lists = ctx.enter_context(tc.tile_pool(name="lists", bufs=1))
+        keep = ctx.enter_context(tc.tile_pool(name="keep", bufs=1))
+        ring = ctx.enter_context(tc.tile_pool(name="ring", bufs=RING))
+        work = ctx.enter_context(tc.tile_pool(name="work", bufs=2))
+        psum = ctx.enter_context(tc.psum_pool(name="psum", bufs=8))
+
+        offs_sb = lists.tile([P, S // 16], U16, name="offs_sb")
+        pos_sb = [lists.tile([P, T // 16], U16, name=f"pos_sb{r}") for r in range(TOP)]
+
+        xs = keep.tile([P, T], U8, name="xs", align_bytes=64)
+        nc.gpsimd.memset(xs[:], 0)
+        warm = keep.tile([P, 1], F32, name="warm")
+        nc.gpsimd.memset(warm[:], 0.0)
+        warm_out = keep.tile([P, 1], F32, name="warm_out")
+        nc.scalar.activation(warm_out[:], warm[:], SILU)
+
+        x_raw = []
+        for half in range(2):
+            xr = keep.tile([P, 4, T // 2], F32, name=f"x_raw{half}")
+            nc.sync.dma_start(out=xr[:], in_=xT.rearrange("(p j) t -> p j t", j=4)[:, :, half * (T // 2) : (half + 1) * (T // 2)])
+            x_raw.append(xr)
+        nc.sync.dma_start(offs_sb[:], offs)
+        raw, gates = {}, {}
+        for kind, e in LOADS:
+            if kind in "ab":
+                wr = ring.tile([P, 4, H], F32, name=f"raw_{kind}{e}", tag="raw")
+                nc.sync.dma_start(out=wr[:], in_=(w1 if kind == "a" else w3)[e].rearrange("(p j) i -> p j i", j=4))
+                raw[kind, e] = wr
+            elif kind == "c":
+                wr = ring.tile([P, 4, N], F32, name=f"raw_c{e}", tag="raw")
+                nc.sync.dma_start(out=wr[:], in_=w2[e].rearrange("(p j) n -> p j n", j=4))
+                for r in range(3):
+                    raw[r, e] = wr[:, :, r * BLK : (r + 1) * BLK]
+            elif kind == "n":
+                wr = keep.tile([P, 4, BLK], F32, name=f"raw_n{e}")
+                nc.sync.dma_start(out=wr[:], in_=w2[e].rearrange("(p j) n -> p j n", j=4)[:, :, 0:BLK])
+                raw[0, e] = wr[:]
+            elif kind == "m":
+                wr = keep.tile([P, 4, 2 * BLK], F32, name=f"raw_m{e}")
+                nc.sync.dma_start(out=wr[:], in_=w2[e].rearrange("(p j) n -> p j n", j=4)[:, :, BLK:N])
+                for r in range(2):
+                    raw[r + 1, e] = wr[:, :, r * BLK : (r + 1) * BLK]
+            else:
+                if e == 0:
+                    for k, src in enumerate((pos1, pos2, pos3)):
+                        nc.sync.dma_start(pos_sb[k][:], src)
+                gt = keep.tile([P, TOP, T], F32, name=f"gate{e}")
+                nc.sync.dma_start(out=gt[:], in_=gate[:, e * BLK : (e + 1) * BLK, :].rearrange("g p t -> p g t"))
+                gates[e] = gt
+
+        def split_copy(dst, src, ms, total):
+            if ms:
+                nc.scalar.copy(dst[:, 0:ms], src[:, 0:ms])
+            if ms < total:
+                nc.vector.tensor_copy(dst[:, ms:total], src[:, ms:total])
+
+        xg = keep.tile([P, T, 4], BF16, name="xg", align_bytes=64)
+        xv = xg[:].rearrange("p (c i) j -> p c j i", i=4)
+        for half in range(2):
+            split_copy(xv[:, half * 64 : (half + 1) * 64], x_raw[half][:].rearrange("p j (c i) -> p c j i", i=4), MSX, 64)
+        xw = keep.tile([P, T], U32, name="xw", align_bytes=64)
+        nc.vector.quantize_mx(out=xw[:].bitcast(FP8X4), scales=xs[:], in_=xg[:].rearrange("p t j -> p (t j)"))
+
+        gw, gs = {}, {}
+
+        def gather(b):
+            cols = slice(b * GATHER // 16, (b + 1) * GATHER // 16)
+            gw[b] = work.tile([P, GATHER], U32, name=f"gw{b}", tag="gw", align_bytes=64, bufs=2)
+            nc.vector.tensor_copy(gw[b][:], xw[:].indirect(offs_sb[:, cols]))
+            gs[b] = work.tile([P, GATHER], U8, name=f"gs{b}", tag="gs", align_bytes=64, bufs=2)
+            nc.vector.tensor_copy(gs[b][:], xs[:].indirect(offs_sb[:, cols]))
+
+        def moving(blk):
+            b, o = divmod(blk * BLK, GATHER)
+            return gw[b][:, o : o + BLK].bitcast(FP8X4), gs[b][:, o : o + BLK]
+
+        w2w, w2s = {}, {}
+
+        def prepare_w2(r):
+            for q in range(3):
+                g = work.tile([P, 2, BLK, 4], BF16, name=f"grp_c{r}_{q}", tag="grp2", align_bytes=64, bufs=4)
+                for u in range(2):
+                    dst = g[:, u].rearrange("p (c i) j -> p c j i", i=4)
+                    split_copy(dst, raw[r, 2 * q + u].rearrange("p j (c i) -> p c j i", i=4), MSN[r], 32)
+                cw = keep.tile([P, 2 * BLK], U32, name=f"cw_c{r}_{q}", align_bytes=64)
+                cs = keep.tile([P, 2 * BLK], U8, name=f"cs_c{r}_{q}", align_bytes=64)
+                nc.vector.quantize_mx(out=cw[:].bitcast(FP8X4), scales=cs[:], in_=g[:].rearrange("p u n j -> p (u n j)"))
+                w2w[r, q], w2s[r, q] = cw, cs
+
+        hw, hs = [], []
+        for e in range(E):
+            for b in GATH.get(e, []):
+                gather(b)
+            codes = []
+            for kind, ms in (("a", MS1[e]), ("b", MS3[e])):
+                g = work.tile([P, 4 * H], BF16, name=f"grp_{kind}{e}", tag="grp", align_bytes=64, bufs=4)
+                split_copy(g[:].rearrange("p (t m j) -> p m j t", t=4, j=4), raw[kind, e][:].rearrange("p j (m t) -> p m j t", t=4), ms, 128)
+                cw = work.tile([P, H], U32, name=f"cw_{kind}{e}", tag="cw", align_bytes=64, bufs=4)
+                cs = work.tile([P, H], U8, name=f"cs_{kind}{e}", tag="cs", align_bytes=64, bufs=4)
+                nc.vector.quantize_mx(out=cw[:].bitcast(FP8X4), scales=cs[:], in_=g[:])
+                codes.append((cw, cs))
+            hb = work.tile([P, C, 4], BF16, name=f"hb{e}", tag="hb", align_bytes=64)
+            for c in range(2):
+                rw, rs = moving(2 * e + c)
+                acc = []
+                for i, (cw, cs) in enumerate(codes):
+                    bank = psum.tile([P, 4, BLK], F32, name=f"bank_{i}_{e}_{c}", tag="bank")
+                    for t in range(4):
+                        sl = slice(t * BLK, (t + 1) * BLK)
+                        nc.tensor.matmul_mx(out=bank[:, t, :], lhsT=cw[:, sl].bitcast(FP8X4), lhsT_scale=cs[:, sl], rhs=rw, rhs_scale=rs, start=True, stop=True)
+                    acc.append(bank)
+                sil = work.tile([P, BLK, 4], F32, name=f"sil{e}_{c}", tag="sil", bufs=3)
+                nc.scalar.activation(sil[:], acc[0][:].rearrange("p t c -> p c t"), SILU)
+                nc.vector.tensor_tensor(hb[:, c * BLK : (c + 1) * BLK, :], acc[1][:].rearrange("p t c -> p c t"), sil[:], MULT)
+            w_ = keep.tile([P, C], U32, name=f"hw{e}", align_bytes=64)
+            s_ = keep.tile([P, C], U8, name=f"hs{e}", align_bytes=64)
+            nc.vector.quantize_mx(out=w_[:].bitcast(FP8X4), scales=s_[:], in_=hb[:].rearrange("p c t -> p (c t)"))
+            hw.append(w_)
+            hs.append(s_)
+            for r in range(3):
+                if POS[r] == e:
+                    prepare_w2(r)
+
+        for r in range(3):
+            y = keep.tile([P, S], F32, name=f"y{r}")
+            for q in range(3):
+                bank = psum.tile([P, 2, C], F32, name=f"bank_y{r}_{q}", tag="bank")
+                for u in range(2):
+                    e = 2 * q + u
+                    sl = slice(u * BLK, (u + 1) * BLK)
+                    nc.tensor.matmul_mx(out=bank[:, u, :], lhsT=w2w[r, q][:, sl].bitcast(FP8X4), lhsT_scale=w2s[r, q][:, sl], rhs=hw[e][:].bitcast(FP8X4), rhs_scale=hs[e][:], start=True, stop=True)
+                if (r, q) in YV:
+                    nc.vector.tensor_copy(y[:, q * 512 : (q + 1) * 512], bank[:].rearrange("p u c -> p (u c)"))
+                else:
+                    nc.scalar.copy(y[:, q * 512 : (q + 1) * 512], bank[:].rearrange("p u c -> p (u c)"))
+            rows = slice(r * BLK, (r + 1) * BLK)
+            prods = [work.tile([P, T], F32, name=f"prod{r}_{k}", tag=f"prod{k}") for k in range(TOP)]
+            s2 = work.tile([P, T], F32, name=f"sum{r}", tag="sum")
+            o = work.tile([P, T], F32, name=f"o{r}", tag="o")
+            for k in range(2):
+                nc.vector.tensor_tensor(prods[k][:], y[:].indirect(pos_sb[k][:]), gates[r][:, k, :], MULT)
+            nc.vector.tensor_tensor(s2[:], prods[0][:], prods[1][:], ADD)
+            pieces = 1 if r < 2 else 2
+            w = T // pieces
+            for h in range(pieces):
+                cols = slice(h * w, (h + 1) * w)
+                nc.vector.tensor_tensor(prods[2][:, cols], y[:].indirect(pos_sb[2][:, h * w // 16 : (h + 1) * w // 16]), gates[r][:, 2, cols], MULT)
+            for h in range(pieces):
+                cols = slice(h * w, (h + 1) * w)
+                nc.vector.tensor_tensor(o[:, cols], s2[:, cols], prods[2][:, cols], ADD)
+                nc.sync.dma_start(out=out[rows, cols], in_=o[:, cols])
+            for rr in range(3):
+                if POS[rr] == 6 + r:
+                    prepare_w2(rr)

@@ -21,16 +21,13 @@ BLK = 128
 GATHER = 384
 S = E * C
 
-MS1 = [80,128,128,128,128,80]
-MS3 = [80,48,48,48,48,80]
-MSX = 40
-MSN = [0,32,32]
-POS = [5,5,6]
-YV = []
-LOADS = [("a", 0), ("b", 0), ("a", 1), ("b", 1), ("a", 2), ("b", 2), ("a", 3), ("b", 3), ("a", 4), ("b", 4), ("a", 5), ("b", 5), ("c", 0), ("c", 1), ("c", 2), ("c", 3), ("n", 4), ("n", 5), ("g", 0), ("m", 4), ("m", 5), ("g", 1), ("g", 2)]
-GATH = {0: [0], 1: [1], 3: [2], 4: [3]}
-RING = 10
-QPAIR = []
+MS1 = [128, 64, 128, 128, 64, 80]
+MS3 = [96, 80, 32, 32, 80, 48]
+MSX = 48
+MSN = [32, 32, 32]
+LOADS = [('a', 0), ('b', 0), ('a', 1), ('b', 1), ('a', 2), ('b', 2), ('c', 0), ('a', 3), ('b', 3), ('c', 1), ('c', 2), ('a', 4), ('b', 4), ('a', 5), ('b', 5), ('n', 3), ('n', 4), ('n', 5), ('g', 0), ('m', 3), ('m', 4), ('m', 5), ('g', 1), ('g', 2)]
+GATH = {0: [0], 1: [1], 2: [2], 3: [3]}
+RING = 13
 
 
 def tile_moe_tk_glu_silu_kernel(tc, xT, w1, w3, w2, gate, offs, pos1, pos2, pos3, out):
@@ -53,12 +50,13 @@ def tile_moe_tk_glu_silu_kernel(tc, xT, w1, w3, w2, gate, offs, pos1, pos2, pos3
         nc.scalar.activation(warm_out[:], warm[:], SILU)
 
         x_raw = []
+        x_all = ring.tile([P, 4, T], F32, name="x_all", tag="raw")
         for half in range(2):
-            xr = keep.tile([P, 4, T // 2], F32, name=f"x_raw{half}")
-            nc.sync.dma_start(out=xr[:], in_=xT.rearrange("(p j) t -> p j t", j=4)[:, :, half * (T // 2) : (half + 1) * (T // 2)])
+            xr = x_all[:, :, half * (T // 2) : (half + 1) * (T // 2)]
+            nc.sync.dma_start(out=xr, in_=xT.rearrange("(p j) t -> p j t", j=4)[:, :, half * (T // 2) : (half + 1) * (T // 2)])
             x_raw.append(xr)
         nc.sync.dma_start(offs_sb[:], offs)
-        raw, gates = {}, {}
+        raw, gates, pieces = {}, {}, {}
         for kind, e in LOADS:
             if kind in "ab":
                 wr = ring.tile([P, 4, H], F32, name=f"raw_{kind}{e}", tag="raw")
@@ -70,19 +68,20 @@ def tile_moe_tk_glu_silu_kernel(tc, xT, w1, w3, w2, gate, offs, pos1, pos2, pos3
                 for r in range(3):
                     raw[r, e] = wr[:, :, r * BLK : (r + 1) * BLK]
             elif kind == "n":
-                wr = keep.tile([P, 4, BLK], F32, name=f"raw_n{e}")
-                nc.sync.dma_start(out=wr[:], in_=w2[e].rearrange("(p j) n -> p j n", j=4)[:, :, 0:BLK])
-                raw[0, e] = wr[:]
+                pieces[e] = ring.tile([P, 4 * N], F32, name=f"raw_nm{e}", tag="raw")
+                wr = pieces[e][:, 0 : 4 * BLK].rearrange("p (j n) -> p j n", j=4)
+                nc.sync.dma_start(out=wr, in_=w2[e].rearrange("(p j) n -> p j n", j=4)[:, :, 0:BLK])
+                raw[0, e] = wr
             elif kind == "m":
-                wr = keep.tile([P, 4, 2 * BLK], F32, name=f"raw_m{e}")
-                nc.sync.dma_start(out=wr[:], in_=w2[e].rearrange("(p j) n -> p j n", j=4)[:, :, BLK:N])
+                wr = pieces[e][:, 4 * BLK : 4 * N].rearrange("p (j n) -> p j n", j=4)
+                nc.sync.dma_start(out=wr, in_=w2[e].rearrange("(p j) n -> p j n", j=4)[:, :, BLK:N])
                 for r in range(2):
                     raw[r + 1, e] = wr[:, :, r * BLK : (r + 1) * BLK]
             else:
                 if e == 0:
                     for k, src in enumerate((pos1, pos2, pos3)):
                         nc.sync.dma_start(pos_sb[k][:], src)
-                gt = keep.tile([P, TOP, T], F32, name=f"gate{e}")
+                gt = ring.tile([P, TOP, T], F32, name=f"gate{e}", tag="raw")
                 nc.sync.dma_start(out=gt[:], in_=gate[:, e * BLK : (e + 1) * BLK, :].rearrange("g p t -> p g t"))
                 gates[e] = gt
 
@@ -95,7 +94,7 @@ def tile_moe_tk_glu_silu_kernel(tc, xT, w1, w3, w2, gate, offs, pos1, pos2, pos3
         xg = keep.tile([P, T, 4], BF16, name="xg", align_bytes=64)
         xv = xg[:].rearrange("p (c i) j -> p c j i", i=4)
         for half in range(2):
-            split_copy(xv[:, half * 64 : (half + 1) * 64], x_raw[half][:].rearrange("p j (c i) -> p c j i", i=4), MSX, 64)
+            split_copy(xv[:, half * 64 : (half + 1) * 64], x_raw[half].rearrange("p j (c i) -> p c j i", i=4), MSX, 64)
         xw = keep.tile([P, T], U32, name="xw", align_bytes=64)
         nc.vector.quantize_mx(out=xw[:].bitcast(FP8X4), scales=xs[:], in_=xg[:].rearrange("p t j -> p (t j)"))
 
@@ -112,81 +111,120 @@ def tile_moe_tk_glu_silu_kernel(tc, xT, w1, w3, w2, gate, offs, pos1, pos2, pos3
             b, o = divmod(blk * BLK, GATHER)
             return gw[b][:, o : o + BLK].bitcast(FP8X4), gs[b][:, o : o + BLK]
 
-        w2w, w2s = {}, {}
+        grouped, codes, hb, hw, hs = {}, {}, {}, {}, {}
+        w2g, w2w, w2s = {}, {}, {}
 
-        def prepare_w2(r):
-            for q in range(3):
-                g = work.tile([P, 2, BLK, 4], BF16, name=f"grp_c{r}_{q}", tag="grp2", align_bytes=64, bufs=4)
-                for u in range(2):
-                    dst = g[:, u].rearrange("p (c i) j -> p c j i", i=4)
-                    split_copy(dst, raw[r, 2 * q + u].rearrange("p j (c i) -> p c j i", i=4), MSN[r], 32)
-                cw = keep.tile([P, 2 * BLK], U32, name=f"cw_c{r}_{q}", align_bytes=64)
-                cs = keep.tile([P, 2 * BLK], U8, name=f"cs_c{r}_{q}", align_bytes=64)
-                nc.vector.quantize_mx(out=cw[:].bitcast(FP8X4), scales=cs[:], in_=g[:].rearrange("p u n j -> p (u n j)"))
-                w2w[r, q], w2s[r, q] = cw, cs
+        def copy_w13(e, i):
+            kind, ms = (("a", MS1[e]), ("b", MS3[e]))[i]
+            grouped[e, i] = work.tile([P, 4 * H], BF16, name=f"grp_{kind}{e}", tag="grp", align_bytes=64, bufs=4)
+            split_copy(grouped[e, i][:].rearrange("p (t m j) -> p m j t", t=4, j=4), raw[kind, e][:].rearrange("p j (m t) -> p m j t", t=4), ms, 128)
 
-        hw, hs = [], []
-        for e in range(E):
-            for b in GATH.get(e, []):
-                gather(b)
-            codes = []
-            for kind, ms in (("a", MS1[e]), ("b", MS3[e])):
-                g = work.tile([P, 4 * H], BF16, name=f"grp_{kind}{e}", tag="grp", align_bytes=64, bufs=4)
-                split_copy(g[:].rearrange("p (t m j) -> p m j t", t=4, j=4), raw[kind, e][:].rearrange("p j (m t) -> p m j t", t=4), ms, 128)
-                cw = work.tile([P, H], U32, name=f"cw_{kind}{e}", tag="cw", align_bytes=64, bufs=4)
-                cs = work.tile([P, H], U8, name=f"cs_{kind}{e}", tag="cs", align_bytes=64, bufs=4)
-                nc.vector.quantize_mx(out=cw[:].bitcast(FP8X4), scales=cs[:], in_=g[:])
-                codes.append((cw, cs))
-            hb = work.tile([P, C, 4], BF16, name=f"hb{e}", tag="hb", align_bytes=64)
+        def quantize_w13(e, i):
+            cw = work.tile([P, H], U32, name=f"cw{e}_{i}", tag="cw", align_bytes=64, bufs=4)
+            cs = work.tile([P, H], U8, name=f"cs{e}_{i}", tag="cs", align_bytes=64, bufs=4)
+            nc.vector.quantize_mx(out=cw[:].bitcast(FP8X4), scales=cs[:], in_=grouped[e, i][:])
+            codes[e, i] = (cw, cs)
+
+        banks = {}
+
+        def hidden(e):
             for c in range(2):
                 rw, rs = moving(2 * e + c)
-                acc = []
-                for i, (cw, cs) in enumerate(codes):
+                for i in range(2):
+                    cw, cs = codes[e, i]
                     bank = psum.tile([P, 4, BLK], F32, name=f"bank_{i}_{e}_{c}", tag="bank")
                     for t in range(4):
                         sl = slice(t * BLK, (t + 1) * BLK)
                         nc.tensor.matmul_mx(out=bank[:, t, :], lhsT=cw[:, sl].bitcast(FP8X4), lhsT_scale=cs[:, sl], rhs=rw, rhs_scale=rs, start=True, stop=True)
-                    acc.append(bank)
-                sil = work.tile([P, BLK, 4], F32, name=f"sil{e}_{c}", tag="sil", bufs=3)
-                nc.scalar.activation(sil[:], acc[0][:].rearrange("p t c -> p c t"), SILU)
-                nc.vector.tensor_tensor(hb[:, c * BLK : (c + 1) * BLK, :], acc[1][:].rearrange("p t c -> p c t"), sil[:], MULT)
-            w_ = keep.tile([P, C], U32, name=f"hw{e}", align_bytes=64)
-            s_ = keep.tile([P, C], U8, name=f"hs{e}", align_bytes=64)
-            nc.vector.quantize_mx(out=w_[:].bitcast(FP8X4), scales=s_[:], in_=hb[:].rearrange("p c t -> p (c t)"))
-            hw.append(w_)
-            hs.append(s_)
-            for r in range(3):
-                if POS[r] == e:
-                    prepare_w2(r)
+                    banks[e, i, c] = bank
 
-        for r in range(3):
-            y = keep.tile([P, S], F32, name=f"y{r}")
+        def activate(e):
+            hb[e] = work.tile([P, C, 4], BF16, name=f"hb{e}", tag="hb", align_bytes=64)
+            if e + 1 < E:
+                room = raw["a", e + 1]
+            else:
+                room = keep.tile([P, 2, H], F32, name="room")
+            for c in range(2):
+                sil = room[:, c, :].rearrange("p (c t) -> p c t", t=4)
+                nc.scalar.activation(sil, banks[e, 0, c][:].rearrange("p t c -> p c t"), SILU)
+                nc.vector.tensor_tensor(hb[e][:, c * BLK : (c + 1) * BLK, :], banks[e, 1, c][:].rearrange("p t c -> p c t"), sil, MULT)
+
+        def quantize_h(e):
+            hw[e] = keep.tile([P, C], U32, name=f"hw{e}", align_bytes=64)
+            hs[e] = keep.tile([P, C], U8, name=f"hs{e}", align_bytes=64)
+            nc.vector.quantize_mx(out=hw[e][:].bitcast(FP8X4), scales=hs[e][:], in_=hb[e][:].rearrange("p c t -> p (c t)"))
+
+        def copy_w2(r, q):
+            w2g[r, q] = keep.tile([P, 2, BLK, 4], BF16, name=f"grp2_{r}_{q}", align_bytes=64)
+            for u in range(2):
+                split_copy(w2g[r, q][:, u].rearrange("p (c i) j -> p c j i", i=4), raw[r, 2 * q + u].rearrange("p j (c i) -> p c j i", i=4), MSN[r], 32)
+
+        def quantize_w2(r, q):
+            w2w[r, q] = keep.tile([P, 2, BLK], U32, name=f"w2w{r}_{q}", align_bytes=64)
+            w2s[r, q] = keep.tile([P, 2, BLK], U8, name=f"w2s{r}_{q}", align_bytes=64)
+            nc.vector.quantize_mx(out=w2w[r, q][:].rearrange("p u n -> p (u n)").bitcast(FP8X4), scales=w2s[r, q][:].rearrange("p u n -> p (u n)"), in_=w2g[r, q][:].rearrange("p u n j -> p (u n j)"))
+
+        ys = {}
+
+        def project(r):
+            ys[r] = keep.tile([P, S], F32, name=f"y{r}")
             for q in range(3):
                 bank = psum.tile([P, 2, C], F32, name=f"bank_y{r}_{q}", tag="bank")
                 for u in range(2):
                     e = 2 * q + u
-                    sl = slice(u * BLK, (u + 1) * BLK)
-                    nc.tensor.matmul_mx(out=bank[:, u, :], lhsT=w2w[r, q][:, sl].bitcast(FP8X4), lhsT_scale=w2s[r, q][:, sl], rhs=hw[e][:].bitcast(FP8X4), rhs_scale=hs[e][:], start=True, stop=True)
-                if (r, q) in YV:
-                    nc.vector.tensor_copy(y[:, q * 512 : (q + 1) * 512], bank[:].rearrange("p u c -> p (u c)"))
-                else:
-                    nc.scalar.copy(y[:, q * 512 : (q + 1) * 512], bank[:].rearrange("p u c -> p (u c)"))
-            rows = slice(r * BLK, (r + 1) * BLK)
-            prods = [work.tile([P, T], F32, name=f"prod{r}_{k}", tag=f"prod{k}") for k in range(TOP)]
-            s2 = work.tile([P, T], F32, name=f"sum{r}", tag="sum")
-            o = work.tile([P, T], F32, name=f"o{r}", tag="o")
-            for k in range(2):
-                nc.vector.tensor_tensor(prods[k][:], y[:].indirect(pos_sb[k][:]), gates[r][:, k, :], MULT)
-            nc.vector.tensor_tensor(s2[:], prods[0][:], prods[1][:], ADD)
-            pieces = 1 if r < 2 else 2
-            w = T // pieces
-            for h in range(pieces):
-                cols = slice(h * w, (h + 1) * w)
-                nc.vector.tensor_tensor(prods[2][:, cols], y[:].indirect(pos_sb[2][:, h * w // 16 : (h + 1) * w // 16]), gates[r][:, 2, cols], MULT)
-            for h in range(pieces):
-                cols = slice(h * w, (h + 1) * w)
-                nc.vector.tensor_tensor(o[:, cols], s2[:, cols], prods[2][:, cols], ADD)
-                nc.sync.dma_start(out=out[rows, cols], in_=o[:, cols])
-            for rr in range(3):
-                if POS[rr] == 6 + r:
-                    prepare_w2(rr)
+                    nc.tensor.matmul_mx(out=bank[:, u, :], lhsT=w2w[r, q][:, u].bitcast(FP8X4), lhsT_scale=w2s[r, q][:, u], rhs=hw[e][:].bitcast(FP8X4), rhs_scale=hs[e][:], start=True, stop=True)
+                nc.scalar.copy(ys[r][:, q * 512 : (q + 1) * 512], bank[:].rearrange("p u c -> p (u c)"))
+
+        prods, sums, outs = {}, {}, {}
+
+        def fetch(r, k, t0=0, t1=T):
+            if (r, k) not in prods:
+                prods[r, k] = work.tile([P, T], F32, name=f"prod{r}_{k}", tag=f"prod{k}")
+            nc.vector.tensor_tensor(prods[r, k][:, t0:t1], ys[r][:].indirect(pos_sb[k][:, t0 // 16 : t1 // 16]), gates[r][:, k, t0:t1], MULT)
+
+        def add01(r):
+            sums[r] = work.tile([P, T], F32, name=f"sum{r}", tag="sum")
+            nc.vector.tensor_tensor(sums[r][:], prods[r, 0][:], prods[r, 1][:], ADD)
+
+        def add2(r, t0=0, t1=T):
+            if r not in outs:
+                outs[r] = work.tile([P, T], F32, name=f"o{r}", tag="o")
+            nc.vector.tensor_tensor(outs[r][:, t0:t1], sums[r][:, t0:t1], prods[r, 2][:, t0:t1], ADD)
+            nc.sync.dma_start(out=out[r * BLK : (r + 1) * BLK, t0:t1], in_=outs[r][:, t0:t1])
+
+        for e in range(E):
+            for b in GATH.get(e, []):
+                gather(b)
+            copy_w13(e, 0)
+            quantize_w13(e, 0)
+            if e > 0:
+                activate(e - 1)
+                quantize_h(e - 1)
+            copy_w13(e, 1)
+            quantize_w13(e, 1)
+            hidden(e)
+        activate(E - 1)
+        quantize_h(E - 1)
+        for q in range(3):
+            for r in range(3):
+                copy_w2(r, q)
+                quantize_w2(r, q)
+        for r in range(3):
+            project(r)
+        fetch(0, 0)
+        fetch(0, 1)
+        fetch(0, 2)
+        add01(0)
+        fetch(1, 0)
+        add2(0)
+        fetch(1, 1)
+        fetch(1, 2)
+        add01(1)
+        fetch(2, 0)
+        add2(1)
+        fetch(2, 1)
+        fetch(2, 2, 0, 256)
+        add01(2)
+        fetch(2, 2, 256, 512)
+        add2(2, 0, 256)
+        add2(2, 256, 512)

@@ -21,13 +21,23 @@ BLK = 128
 GATHER = 384
 S = E * C
 
-MS1 = [128, 64, 128, 128, 64, 80]
-MS3 = [96, 80, 32, 32, 80, 48]
-MSX = 48
-MSN = [32, 32, 32]
-LOADS = [('a', 0), ('b', 0), ('a', 1), ('b', 1), ('a', 2), ('b', 2), ('c', 0), ('a', 3), ('b', 3), ('c', 1), ('c', 2), ('a', 4), ('b', 4), ('a', 5), ('b', 5), ('n', 3), ('n', 4), ('n', 5), ('g', 0), ('m', 3), ('m', 4), ('m', 5), ('g', 1), ('g', 2)]
+MS1 = [128, 96, 128, 96, 80, 64]
+MS3 = [96, 112, 48, 32, 64, 64]
+MSX = 40
+MSN = [[8, 24, 0], [16, 0, 0], [16, 32, 32]]
+LOADS = [('a', 0), ('b', 0), ('a', 1), ('b', 1), ('c', 1), ('a', 2), ('b', 2), ('a', 3), ('b', 3), ('c', 0), ('a', 4), ('b', 4), ('c', 2), ('a', 5), ('b', 5), ('n', 3), ('n', 4), ('n', 5), ('g', 0), ('m', 3), ('m', 4), ('m', 5), ('g', 1), ('g', 2)]
 GATH = {0: [0], 1: [1], 2: [2], 3: [3]}
-RING = 13
+RING = 12
+GB = 3
+XPOS = 0
+ROOM = 'baaaa'
+YV = []
+PAIRS = [(0, 1), (2, 5), (3, 4)]
+HALVES = [('b', 5)]
+YROOM = 0
+QA = 1
+ENDORD = 1
+LATE = [(2, 0), (1, 0), (1, 2)]
 
 
 def tile_moe_tk_glu_silu_kernel(tc, xT, w1, w3, w2, gate, offs, pos1, pos2, pos3, out):
@@ -50,17 +60,23 @@ def tile_moe_tk_glu_silu_kernel(tc, xT, w1, w3, w2, gate, offs, pos1, pos2, pos3
         nc.scalar.activation(warm_out[:], warm[:], SILU)
 
         x_raw = []
-        x_all = ring.tile([P, 4, T], F32, name="x_all", tag="raw")
-        for half in range(2):
-            xr = x_all[:, :, half * (T // 2) : (half + 1) * (T // 2)]
-            nc.sync.dma_start(out=xr, in_=xT.rearrange("(p j) t -> p j t", j=4)[:, :, half * (T // 2) : (half + 1) * (T // 2)])
-            x_raw.append(xr)
-        nc.sync.dma_start(offs_sb[:], offs)
         raw, gates, pieces = {}, {}, {}
-        for kind, e in LOADS:
+        for n, (kind, e) in enumerate(LOADS):
+            if n == XPOS:
+                x_all = ring.tile([P, 4, T], F32, name="x_all", tag="raw")
+                for half in range(2):
+                    xr = x_all[:, :, half * (T // 2) : (half + 1) * (T // 2)]
+                    nc.sync.dma_start(out=xr, in_=xT.rearrange("(p j) t -> p j t", j=4)[:, :, half * (T // 2) : (half + 1) * (T // 2)])
+                    x_raw.append(xr)
+                nc.sync.dma_start(offs_sb[:], offs)
             if kind in "ab":
                 wr = ring.tile([P, 4, H], F32, name=f"raw_{kind}{e}", tag="raw")
-                nc.sync.dma_start(out=wr[:], in_=(w1 if kind == "a" else w3)[e].rearrange("(p j) i -> p j i", j=4))
+                src = (w1 if kind == "a" else w3)[e].rearrange("(p j) i -> p j i", j=4)
+                if (kind, e) in HALVES:
+                    nc.sync.dma_start(out=wr[:, :, 0:256], in_=src[:, :, 0:256])
+                    nc.sync.dma_start(out=wr[:, :, 256:512], in_=src[:, :, 256:512])
+                else:
+                    nc.sync.dma_start(out=wr[:], in_=src)
                 raw[kind, e] = wr
             elif kind == "c":
                 wr = ring.tile([P, 4, N], F32, name=f"raw_c{e}", tag="raw")
@@ -102,9 +118,9 @@ def tile_moe_tk_glu_silu_kernel(tc, xT, w1, w3, w2, gate, offs, pos1, pos2, pos3
 
         def gather(b):
             cols = slice(b * GATHER // 16, (b + 1) * GATHER // 16)
-            gw[b] = work.tile([P, GATHER], U32, name=f"gw{b}", tag="gw", align_bytes=64, bufs=2)
+            gw[b] = work.tile([P, GATHER], U32, name=f"gw{b}", tag="gw", align_bytes=64, bufs=GB)
             nc.vector.tensor_copy(gw[b][:], xw[:].indirect(offs_sb[:, cols]))
-            gs[b] = work.tile([P, GATHER], U8, name=f"gs{b}", tag="gs", align_bytes=64, bufs=2)
+            gs[b] = work.tile([P, GATHER], U8, name=f"gs{b}", tag="gs", align_bytes=64, bufs=GB)
             nc.vector.tensor_copy(gs[b][:], xs[:].indirect(offs_sb[:, cols]))
 
         def moving(blk):
@@ -141,9 +157,9 @@ def tile_moe_tk_glu_silu_kernel(tc, xT, w1, w3, w2, gate, offs, pos1, pos2, pos3
         def activate(e):
             hb[e] = work.tile([P, C, 4], BF16, name=f"hb{e}", tag="hb", align_bytes=64)
             if e + 1 < E:
-                room = raw["a", e + 1]
+                room = raw[ROOM[e], e + 1]
             else:
-                room = keep.tile([P, 2, H], F32, name="room")
+                room = work.tile([P, 2, H], F32, name="room", tag="room", align_bytes=64, bufs=1)
             for c in range(2):
                 sil = room[:, c, :].rearrange("p (c t) -> p c t", t=4)
                 nc.scalar.activation(sil, banks[e, 0, c][:].rearrange("p t c -> p c t"), SILU)
@@ -154,26 +170,41 @@ def tile_moe_tk_glu_silu_kernel(tc, xT, w1, w3, w2, gate, offs, pos1, pos2, pos3
             hs[e] = keep.tile([P, C], U8, name=f"hs{e}", align_bytes=64)
             nc.vector.quantize_mx(out=hw[e][:].bitcast(FP8X4), scales=hs[e][:], in_=hb[e][:].rearrange("p c t -> p (c t)"))
 
+        late = []
+
         def copy_w2(r, q):
-            w2g[r, q] = keep.tile([P, 2, BLK, 4], BF16, name=f"grp2_{r}_{q}", align_bytes=64)
+            if (r, q) in LATE:
+                if not late:
+                    late.append(work.tile([P, 6, 2, BLK, 4], BF16, name="late", tag="room", align_bytes=64, bufs=1))
+                w2g[r, q] = late[0][:, 3 * (r - 1) + q]
+            else:
+                w2g[r, q] = keep.tile([P, 2, BLK, 4], BF16, name=f"grp2_{r}_{q}", align_bytes=64)[:]
             for u in range(2):
-                split_copy(w2g[r, q][:, u].rearrange("p (c i) j -> p c j i", i=4), raw[r, 2 * q + u].rearrange("p j (c i) -> p c j i", i=4), MSN[r], 32)
+                split_copy(w2g[r, q][:, u].rearrange("p (c i) j -> p c j i", i=4), raw[r, PAIRS[q][u]].rearrange("p j (c i) -> p c j i", i=4), MSN[r][q], 32)
 
         def quantize_w2(r, q):
             w2w[r, q] = keep.tile([P, 2, BLK], U32, name=f"w2w{r}_{q}", align_bytes=64)
             w2s[r, q] = keep.tile([P, 2, BLK], U8, name=f"w2s{r}_{q}", align_bytes=64)
-            nc.vector.quantize_mx(out=w2w[r, q][:].rearrange("p u n -> p (u n)").bitcast(FP8X4), scales=w2s[r, q][:].rearrange("p u n -> p (u n)"), in_=w2g[r, q][:].rearrange("p u n j -> p (u n j)"))
+            nc.vector.quantize_mx(out=w2w[r, q][:].rearrange("p u n -> p (u n)").bitcast(FP8X4), scales=w2s[r, q][:].rearrange("p u n -> p (u n)"), in_=w2g[r, q].rearrange("p u n j -> p (u n j)"))
 
         ys = {}
 
         def project(r):
-            ys[r] = keep.tile([P, S], F32, name=f"y{r}")
+            if r == 0 and YROOM:
+                ys[r] = work.tile([P, S], F32, name=f"y{r}", tag="room", align_bytes=64, bufs=1)
+            else:
+                ys[r] = keep.tile([P, S], F32, name=f"y{r}")
             for q in range(3):
                 bank = psum.tile([P, 2, C], F32, name=f"bank_y{r}_{q}", tag="bank")
                 for u in range(2):
-                    e = 2 * q + u
+                    e = PAIRS[q][u]
                     nc.tensor.matmul_mx(out=bank[:, u, :], lhsT=w2w[r, q][:, u].bitcast(FP8X4), lhsT_scale=w2s[r, q][:, u], rhs=hw[e][:].bitcast(FP8X4), rhs_scale=hs[e][:], start=True, stop=True)
-                nc.scalar.copy(ys[r][:, q * 512 : (q + 1) * 512], bank[:].rearrange("p u c -> p (u c)"))
+                e0, e1 = PAIRS[q]
+                dst = ys[r][:].rearrange("p (e c) -> p e c", c=C)[:, e0 : e1 + 1 : e1 - e0]
+                if (r, q) in YV:
+                    nc.vector.tensor_copy(dst, bank[:])
+                else:
+                    nc.scalar.copy(dst, bank[:])
 
         prods, sums, outs = {}, {}, {}
 
@@ -196,21 +227,29 @@ def tile_moe_tk_glu_silu_kernel(tc, xT, w1, w3, w2, gate, offs, pos1, pos2, pos3
             for b in GATH.get(e, []):
                 gather(b)
             copy_w13(e, 0)
-            quantize_w13(e, 0)
-            if e > 0:
+            if not QA:
+                quantize_w13(e, 0)
+            if e > 0 and ROOM[e - 1] == "a":
                 activate(e - 1)
                 quantize_h(e - 1)
+            if QA:
+                quantize_w13(e, 0)
             copy_w13(e, 1)
             quantize_w13(e, 1)
+            if e > 0 and ROOM[e - 1] == "b":
+                activate(e - 1)
+                quantize_h(e - 1)
             hidden(e)
         activate(E - 1)
         quantize_h(E - 1)
-        for q in range(3):
+        for r, q in [(r, q) for q in range(3) for r in range(3)] if ENDORD == 0 else [(r, q) for r in range(3) for q in range(3)]:
+            copy_w2(r, q)
+            quantize_w2(r, q)
+            if ENDORD == 2 and q == 2:
+                project(r)
+        if ENDORD < 2:
             for r in range(3):
-                copy_w2(r, q)
-                quantize_w2(r, q)
-        for r in range(3):
-            project(r)
+                project(r)
         fetch(0, 0)
         fetch(0, 1)
         fetch(0, 2)

@@ -21,23 +21,24 @@ BLK = 128
 GATHER = 384
 S = E * C
 
-MS1 = [128, 96, 128, 96, 80, 64]
-MS3 = [96, 112, 48, 32, 64, 64]
-MSX = 40
-MSN = [[8, 24, 0], [16, 0, 0], [16, 32, 32]]
-LOADS = [('a', 0), ('b', 0), ('a', 1), ('b', 1), ('c', 1), ('a', 2), ('b', 2), ('a', 3), ('b', 3), ('c', 0), ('a', 4), ('b', 4), ('c', 2), ('a', 5), ('b', 5), ('n', 3), ('n', 4), ('n', 5), ('g', 0), ('m', 3), ('m', 4), ('m', 5), ('g', 1), ('g', 2)]
-GATH = {0: [0], 1: [1], 2: [2], 3: [3]}
-RING = 12
+MS1 = [112, 128, 128, 128, 96, 112]
+MS3 = [128, 80, 32, 64, 48, 128]
+MSX = 32
+MSN = [[32, 32, 0], [8, 0, 32], [8, 16, 8]]
+LOADS = [('a', 0), ('b', 0), ('a', 1), ('b', 1), ('b', 2), ('a', 3), ('a', 2), ('b', 3), ('a', 4), ('b', 4), ('b', 5), ('c', 1), ('c', 0), ('a', 5), ('n', 5), ('c', 3), ('n', 2), ('c', 4), ('m', 5), ('m', 2), ('g', 0), ('g', 1), ('g', 2)]
+GATH = {0: [0, 1], 3: [2], 4: [3]}
+RING = 11
 GB = 3
 XPOS = 0
 ROOM = 'baaaa'
 YV = []
-PAIRS = [(0, 1), (2, 5), (3, 4)]
-HALVES = [('b', 5)]
+PAIRS = [(0, 1), (2, 3), (4, 5)]
+HALVES = []
 YROOM = 0
-QA = 1
-ENDORD = 1
-LATE = [(2, 0), (1, 0), (1, 2)]
+QA = 0
+ENDORD = 0
+LATE = []
+XH = 1
 
 
 def tile_moe_tk_glu_silu_kernel(tc, xT, w1, w3, w2, gate, offs, pos1, pos2, pos3, out):
@@ -64,9 +65,9 @@ def tile_moe_tk_glu_silu_kernel(tc, xT, w1, w3, w2, gate, offs, pos1, pos2, pos3
         for n, (kind, e) in enumerate(LOADS):
             if n == XPOS:
                 x_all = ring.tile([P, 4, T], F32, name="x_all", tag="raw")
-                for half in range(2):
-                    xr = x_all[:, :, half * (T // 2) : (half + 1) * (T // 2)]
-                    nc.sync.dma_start(out=xr, in_=xT.rearrange("(p j) t -> p j t", j=4)[:, :, half * (T // 2) : (half + 1) * (T // 2)])
+                for half in range(XH):
+                    xr = x_all[:, :, half * (T // XH) : (half + 1) * (T // XH)]
+                    nc.sync.dma_start(out=xr, in_=xT.rearrange("(p j) t -> p j t", j=4)[:, :, half * (T // XH) : (half + 1) * (T // XH)])
                     x_raw.append(xr)
                 nc.sync.dma_start(offs_sb[:], offs)
             if kind in "ab":
@@ -109,8 +110,9 @@ def tile_moe_tk_glu_silu_kernel(tc, xT, w1, w3, w2, gate, offs, pos1, pos2, pos3
 
         xg = keep.tile([P, T, 4], BF16, name="xg", align_bytes=64)
         xv = xg[:].rearrange("p (c i) j -> p c j i", i=4)
-        for half in range(2):
-            split_copy(xv[:, half * 64 : (half + 1) * 64], x_raw[half].rearrange("p j (c i) -> p c j i", i=4), MSX, 64)
+        w = T // 4 // XH
+        for half in range(XH):
+            split_copy(xv[:, half * w : (half + 1) * w], x_raw[half].rearrange("p j (c i) -> p c j i", i=4), MSX * w // 64, w)
         xw = keep.tile([P, T], U32, name="xw", align_bytes=64)
         nc.vector.quantize_mx(out=xw[:].bitcast(FP8X4), scales=xs[:], in_=xg[:].rearrange("p t j -> p (t j)"))
 

from contextlib import ExitStack

import concourse.mybir as mybir

K, T, E, C, H, N = 512, 512, 6, 256, 512, 384
TOP = 3
FLOPS = 2 * TOP * T * (2 * K * H + H * N)

F32 = mybir.dt.float32
BF16 = mybir.dt.bfloat16
U32 = mybir.dt.uint32
U16 = mybir.dt.uint16
U8 = mybir.dt.uint8
FP8X4 = mybir.dt.float8_e4m3fn_x4
MULT = mybir.AluOpType.mult
ADD = mybir.AluOpType.add
SILU = mybir.ActivationFunctionType.Silu

P = 128
BLK = 128
GATHER = 384
S = E * C

MS1 = [112, 128, 128, 128, 96, 112]
MS3 = [128, 80, 32, 64, 48, 128]
MSX = 32
MSN = [[32, 32, 0], [8, 0, 32], [8, 16, 8]]
LOADS = [('a', 0), ('b', 0), ('a', 1), ('b', 1), ('b', 2), ('a', 3), ('a', 2), ('b', 3), ('a', 4), ('b', 4), ('b', 5), ('c', 1), ('c', 0), ('a', 5), ('n', 5), ('c', 3), ('n', 2), ('c', 4), ('m', 5), ('m', 2), ('g', 0), ('g', 1), ('g', 2)]
GATH = {0: [0, 1], 3: [2], 4: [3]}
RING = 11
GB = 3
XPOS = 0
ROOM = 'baaaa'
YV = []
PAIRS = [(0, 1), (2, 3), (4, 5)]
HALVES = []
YROOM = 0
QA = 0
ENDORD = 0
LATE = []
XH = 1


def tile_moe_tk_glu_silu_kernel(tc, xT, w1, w3, w2, gate, offs, pos1, pos2, pos3, out):
    nc = tc.nc
    with ExitStack() as ctx:
        lists = ctx.enter_context(tc.tile_pool(name="lists", bufs=1))
        keep = ctx.enter_context(tc.tile_pool(name="keep", bufs=1))
        ring = ctx.enter_context(tc.tile_pool(name="ring", bufs=RING))
        work = ctx.enter_context(tc.tile_pool(name="work", bufs=2))
        psum = ctx.enter_context(tc.psum_pool(name="psum", bufs=8))

        offs_sb = lists.tile([P, S // 16], U16, name="offs_sb")
        pos_sb = [lists.tile([P, T // 16], U16, name=f"pos_sb{r}") for r in range(TOP)]

        xs = keep.tile([P, T], U8, name="xs", align_bytes=64)
        nc.gpsimd.memset(xs[:], 0)
        warm = keep.tile([P, 1], F32, name="warm")
        nc.gpsimd.memset(warm[:], 0.0)
        warm_out = keep.tile([P, 1], F32, name="warm_out")
        nc.scalar.activation(warm_out[:], warm[:], SILU)

        x_raw = []
        raw, gates, pieces = {}, {}, {}
        for n, (kind, e) in enumerate(LOADS):
            if n == XPOS:
                x_all = ring.tile([P, 4, T], F32, name="x_all", tag="raw")
                for half in range(XH):
                    xr = x_all[:, :, half * (T // XH) : (half + 1) * (T // XH)]
                    nc.sync.dma_start(out=xr, in_=xT.rearrange("(p j) t -> p j t", j=4)[:, :, half * (T // XH) : (half + 1) * (T // XH)])
                    x_raw.append(xr)
                nc.sync.dma_start(offs_sb[:], offs)
            if kind in "ab":
                wr = ring.tile([P, 4, H], F32, name=f"raw_{kind}{e}", tag="raw")
                src = (w1 if kind == "a" else w3)[e].rearrange("(p j) i -> p j i", j=4)
                if (kind, e) in HALVES:
                    nc.sync.dma_start(out=wr[:, :, 0:256], in_=src[:, :, 0:256])
                    nc.sync.dma_start(out=wr[:, :, 256:512], in_=src[:, :, 256:512])
                else:
                    nc.sync.dma_start(out=wr[:], in_=src)
                raw[kind, e] = wr
            elif kind == "c":
                wr = ring.tile([P, 4, N], F32, name=f"raw_c{e}", tag="raw")
                nc.sync.dma_start(out=wr[:], in_=w2[e].rearrange("(p j) n -> p j n", j=4))
                for r in range(3):
                    raw[r, e] = wr[:, :, r * BLK : (r + 1) * BLK]
            elif kind == "n":
                pieces[e] = ring.tile([P, 4 * N], F32, name=f"raw_nm{e}", tag="raw")
                wr = pieces[e][:, 0 : 4 * BLK].rearrange("p (j n) -> p j n", j=4)
                nc.sync.dma_start(out=wr, in_=w2[e].rearrange("(p j) n -> p j n", j=4)[:, :, 0:BLK])
                raw[0, e] = wr
            elif kind == "m":
                wr = pieces[e][:, 4 * BLK : 4 * N].rearrange("p (j n) -> p j n", j=4)
                nc.sync.dma_start(out=wr, in_=w2[e].rearrange("(p j) n -> p j n", j=4)[:, :, BLK:N])
                for r in range(2):
                    raw[r + 1, e] = wr[:, :, r * BLK : (r + 1) * BLK]
            else:
                if e == 0:
                    for k, src in enumerate((pos1, pos2, pos3)):
                        nc.sync.dma_start(pos_sb[k][:], src)
                gt = ring.tile([P, TOP, T], F32, name=f"gate{e}", tag="raw")
                nc.sync.dma_start(out=gt[:], in_=gate[:, e * BLK : (e + 1) * BLK, :].rearrange("g p t -> p g t"))
                gates[e] = gt

        def split_copy(dst, src, ms, total):
            if ms:
                nc.scalar.copy(dst[:, 0:ms], src[:, 0:ms])
            if ms < total:
                nc.vector.tensor_copy(dst[:, ms:total], src[:, ms:total])

        xg = keep.tile([P, T, 4], BF16, name="xg", align_bytes=64)
        xv = xg[:].rearrange("p (c i) j -> p c j i", i=4)
        w = T // 4 // XH
        for half in range(XH):
            split_copy(xv[:, half * w : (half + 1) * w], x_raw[half].rearrange("p j (c i) -> p c j i", i=4), MSX * w // 64, w)
        xw = keep.tile([P, T], U32, name="xw", align_bytes=64)
        nc.vector.quantize_mx(out=xw[:].bitcast(FP8X4), scales=xs[:], in_=xg[:].rearrange("p t j -> p (t j)"))

        gw, gs = {}, {}

        def gather(b):
            cols = slice(b * GATHER // 16, (b + 1) * GATHER // 16)
            gw[b] = work.tile([P, GATHER], U32, name=f"gw{b}", tag="gw", align_bytes=64, bufs=GB)
            nc.vector.tensor_copy(gw[b][:], xw[:].indirect(offs_sb[:, cols]))
            gs[b] = work.tile([P, GATHER], U8, name=f"gs{b}", tag="gs", align_bytes=64, bufs=GB)
            nc.vector.tensor_copy(gs[b][:], xs[:].indirect(offs_sb[:, cols]))

        def moving(blk):
            b, o = divmod(blk * BLK, GATHER)
            return gw[b][:, o : o + BLK].bitcast(FP8X4), gs[b][:, o : o + BLK]

        grouped, codes, hb, hw, hs = {}, {}, {}, {}, {}
        w2g, w2w, w2s = {}, {}, {}

        def copy_w13(e, i):
            kind, ms = (("a", MS1[e]), ("b", MS3[e]))[i]
            grouped[e, i] = work.tile([P, 4 * H], BF16, name=f"grp_{kind}{e}", tag="grp", align_bytes=64, bufs=4)
            split_copy(grouped[e, i][:].rearrange("p (t m j) -> p m j t", t=4, j=4), raw[kind, e][:].rearrange("p j (m t) -> p m j t", t=4), ms, 128)

        def quantize_w13(e, i):
            cw = work.tile([P, H], U32, name=f"cw{e}_{i}", tag="cw", align_bytes=64, bufs=4)
            cs = work.tile([P, H], U8, name=f"cs{e}_{i}", tag="cs", align_bytes=64, bufs=4)
            nc.vector.quantize_mx(out=cw[:].bitcast(FP8X4), scales=cs[:], in_=grouped[e, i][:])
            codes[e, i] = (cw, cs)

        banks = {}

        def hidden(e):
            for c in range(2):
                rw, rs = moving(2 * e + c)
                for i in range(2):
                    cw, cs = codes[e, i]
                    bank = psum.tile([P, 4, BLK], F32, name=f"bank_{i}_{e}_{c}", tag="bank")
                    for t in range(4):
                        sl = slice(t * BLK, (t + 1) * BLK)
                        nc.tensor.matmul_mx(out=bank[:, t, :], lhsT=cw[:, sl].bitcast(FP8X4), lhsT_scale=cs[:, sl], rhs=rw, rhs_scale=rs, start=True, stop=True)
                    banks[e, i, c] = bank

        def activate(e):
            hb[e] = work.tile([P, C, 4], BF16, name=f"hb{e}", tag="hb", align_bytes=64)
            if e + 1 < E:
                room = raw[ROOM[e], e + 1]
            else:
                room = work.tile([P, 2, H], F32, name="room", tag="room", align_bytes=64, bufs=1)
            for c in range(2):
                sil = room[:, c, :].rearrange("p (c t) -> p c t", t=4)
                nc.scalar.activation(sil, banks[e, 0, c][:].rearrange("p t c -> p c t"), SILU)
                nc.vector.tensor_tensor(hb[e][:, c * BLK : (c + 1) * BLK, :], banks[e, 1, c][:].rearrange("p t c -> p c t"), sil, MULT)

        def quantize_h(e):
            hw[e] = keep.tile([P, C], U32, name=f"hw{e}", align_bytes=64)
            hs[e] = keep.tile([P, C], U8, name=f"hs{e}", align_bytes=64)
            nc.vector.quantize_mx(out=hw[e][:].bitcast(FP8X4), scales=hs[e][:], in_=hb[e][:].rearrange("p c t -> p (c t)"))

        late = []

        def copy_w2(r, q):
            if (r, q) in LATE:
                if not late:
                    late.append(work.tile([P, 6, 2, BLK, 4], BF16, name="late", tag="room", align_bytes=64, bufs=1))
                w2g[r, q] = late[0][:, 3 * (r - 1) + q]
            else:
                w2g[r, q] = keep.tile([P, 2, BLK, 4], BF16, name=f"grp2_{r}_{q}", align_bytes=64)[:]
            for u in range(2):
                split_copy(w2g[r, q][:, u].rearrange("p (c i) j -> p c j i", i=4), raw[r, PAIRS[q][u]].rearrange("p j (c i) -> p c j i", i=4), MSN[r][q], 32)

        def quantize_w2(r, q):
            w2w[r, q] = keep.tile([P, 2, BLK], U32, name=f"w2w{r}_{q}", align_bytes=64)
            w2s[r, q] = keep.tile([P, 2, BLK], U8, name=f"w2s{r}_{q}", align_bytes=64)
            nc.vector.quantize_mx(out=w2w[r, q][:].rearrange("p u n -> p (u n)").bitcast(FP8X4), scales=w2s[r, q][:].rearrange("p u n -> p (u n)"), in_=w2g[r, q].rearrange("p u n j -> p (u n j)"))

        ys = {}

        def project(r):
            if r == 0 and YROOM:
                ys[r] = work.tile([P, S], F32, name=f"y{r}", tag="room", align_bytes=64, bufs=1)
            else:
                ys[r] = keep.tile([P, S], F32, name=f"y{r}")
            for q in range(3):
                bank = psum.tile([P, 2, C], F32, name=f"bank_y{r}_{q}", tag="bank")
                for u in range(2):
                    e = PAIRS[q][u]
                    nc.tensor.matmul_mx(out=bank[:, u, :], lhsT=w2w[r, q][:, u].bitcast(FP8X4), lhsT_scale=w2s[r, q][:, u], rhs=hw[e][:].bitcast(FP8X4), rhs_scale=hs[e][:], start=True, stop=True)
                e0, e1 = PAIRS[q]
                dst = ys[r][:].rearrange("p (e c) -> p e c", c=C)[:, e0 : e1 + 1 : e1 - e0]
                if (r, q) in YV:
                    nc.vector.tensor_copy(dst, bank[:])
                else:
                    nc.scalar.copy(dst, bank[:])

        prods, sums, outs = {}, {}, {}

        def fetch(r, k, t0=0, t1=T):
            if (r, k) not in prods:
                prods[r, k] = work.tile([P, T], F32, name=f"prod{r}_{k}", tag=f"prod{k}")
            nc.vector.tensor_tensor(prods[r, k][:, t0:t1], ys[r][:].indirect(pos_sb[k][:, t0 // 16 : t1 // 16]), gates[r][:, k, t0:t1], MULT)

        def add01(r):
            sums[r] = work.tile([P, T], F32, name=f"sum{r}", tag="sum")
            nc.vector.tensor_tensor(sums[r][:], prods[r, 0][:], prods[r, 1][:], ADD)

        def add2(r, t0=0, t1=T):
            if r not in outs:
                outs[r] = work.tile([P, T], F32, name=f"o{r}", tag="o")
            nc.vector.tensor_tensor(outs[r][:, t0:t1], sums[r][:, t0:t1], prods[r, 2][:, t0:t1], ADD)
            nc.sync.dma_start(out=out[r * BLK : (r + 1) * BLK, t0:t1], in_=outs[r][:, t0:t1])

        for e in range(E):
            for b in GATH.get(e, []):
                gather(b)
            copy_w13(e, 0)
            if not QA:
                quantize_w13(e, 0)
            if e > 0 and ROOM[e - 1] == "a":
                activate(e - 1)
                quantize_h(e - 1)
            if QA:
                quantize_w13(e, 0)
            copy_w13(e, 1)
            quantize_w13(e, 1)
            if e > 0 and ROOM[e - 1] == "b":
                activate(e - 1)
                quantize_h(e - 1)
            hidden(e)
        activate(E - 1)
        quantize_h(E - 1)
        for r, q in [(r, q) for q in range(3) for r in range(3)] if ENDORD == 0 else [(r, q) for r in range(3) for q in range(3)]:
            copy_w2(r, q)
            quantize_w2(r, q)
            if ENDORD == 2 and q == 2:
                project(r)
        if ENDORD < 2:
            for r in range(3):
                project(r)
        fetch(0, 0)
        fetch(0, 1)
        fetch(0, 2)
        add01(0)
        fetch(1, 0)
        add2(0)
        fetch(1, 1)
        fetch(1, 2)
        add01(1)
        fetch(2, 0)
        add2(1)
        fetch(2, 1)
        fetch(2, 2, 0, 256)
        add01(2)
        fetch(2, 2, 256, 512)
        add2(2, 0, 256)
        add2(2, 256, 512)
